import numpy as np, ml_dtypes
CORES = [66,74,82,90,194,202,210,218]
N = 8
import mx_ref
BF = ml_dtypes.bfloat16
def pick(q, e):
    c = np.concatenate([q[0].reshape(128, -1, 4), np.zeros((128, 1, 4), np.uint8)], axis=1); s = np.concatenate([q[1], np.ones((16, 1), np.uint8)], axis=1)
    return (np.ascontiguousarray(c[:, e].reshape(128, -1)), np.ascontiguousarray(s[:, e]))
def join(*qs):
    return (np.concatenate([q[0] for q in qs], axis=1), np.concatenate([q[1] for q in qs], axis=1))
def put(q, e, v):
    c, s = q[0].reshape(128, -1, 4).copy(), q[1].copy(); c[:, e] = v[0].reshape(128, -1, 4); s[:, e] = v[1]
    return (c.reshape(128, -1), s)
def pk(c, s):
    return (np.ascontiguousarray(c), mx_ref.live(s))
def emit(q):
    return q[0], q[1]
def decode(q):
    o = []
    for b in range(4):
        e = np.zeros((128, 128, 4), np.float32); e[np.arange(128), np.arange(128), b] = 1
        o.append(mx_ref.matmul(mx_ref.quantize(e.reshape(128, 512).astype(BF)), q))
    return np.stack(o, axis=2).reshape(128, -1)
def f(rng, *shape):
    return mx_ref.flush((rng.standard_normal(shape, dtype=np.float32) * np.exp2(rng.integers(-2, 3, shape[:-1] + (1,)))).astype(BF))
def wide(rng, *shape, cols=0):
    v = rng.standard_normal(shape, dtype=np.float32) * np.exp2(rng.integers(-12, 13, shape)).astype(np.float32)
    if cols: v *= np.repeat(np.exp2(rng.integers(-cols, cols + 1, shape[:-2] + (1, shape[-1] // 4))) * (rng.random(shape[:-2] + (1, shape[-1] // 4)) > 0.0625), 4, axis=-1).astype(np.float32)
    return mx_ref.flush(v.astype(BF))
P, K, R = 96, 16, 3
def lift(v):
    v = np.asarray(v).astype(np.float32)
    v[np.abs(v) < np.float32(2.0 ** -16)] = 0
    return v.astype(BF)
def whole(x, hc, u, w):
    i = np.arange(N)
    return {"x": x, "hl": hc[(i - 1) % N], "hc": hc, "hr": hc[(i + 1) % N], "u": u, "w": w}
def query(rng):
    v = np.zeros((N, 128, 512), BF)
    v[:, :, :4] = f(rng, 128, 4)
    return v
def near(rng, hc):
    k = np.repeat(np.exp2(rng.integers(-3, 2, (N, 1, P))), 4, axis=2)
    return lift(hc.astype(np.float32) + f(rng, N, 128, 4 * P).astype(np.float32) * k)
def setup_inputs(rng):
    hc = lift(f(rng, N, 128, 4 * P))
    return whole(near(rng, hc), hc, query(rng), f(rng, N, 128, 512))
def setup_inputs_spread(rng):
    hc = lift(wide(rng, N, 128, 4 * P, cols=4))
    return whole(lift(wide(rng, N, 128, 4 * P, cols=4)), hc, query(rng), f(rng, N, 128, 512))
def setup_inputs_ties(rng):
    d = setup_inputs(rng)
    g = rng.permutation(P) // 7
    s = np.repeat(1 - 2 * rng.integers(0, 2, P), 4).astype(np.float32)
    def same(v):
        return (v.reshape(N, 128, P, 4)[:, :, g].reshape(N, 128, 4 * P).astype(np.float32) * s).astype(BF)
    return whole(same(d["x"]), same(d["hc"]), d["u"], d["w"])
def setup_inputs_again(rng):
    d = setup_inputs(rng)
    k = np.ones(P, np.float32)
    k[rng.permutation(P)[:K]] = 1024
    k = np.repeat(k, 4)
    return whole(lift(d["x"].astype(np.float32) * k), lift(d["hc"].astype(np.float32) * k), d["u"], d["w"])
def setup_inputs_still(rng):
    d = setup_inputs(rng)
    v = rng.integers(128, 256, (16, 8, P, 4)) * np.exp2(rng.integers(-10, -7, (16, 8, P, 4)))
    v[:, 0, :, 0] = (128 + 8 * np.argsort(rng.random((16, P)), axis=0) + rng.integers(1, 8, (16, P))) * 2.0 ** -7
    v = v * rng.choice([-1.0, 1.0], v.shape) * np.exp2(rng.integers(-2, 3, (16, 1, P, 1)))
    v = v.reshape(128, 4 * P).astype(np.float32).astype(BF)
    held = decode(mx_ref.quantize(v)).astype(BF)
    s = int(rng.integers(0, N))
    hc = np.array(d["hc"])
    for r in range(s - 1, s + 3): hc[r % N] = v
    x = near(rng, hc)
    x[s] = held
    few = np.array(x[(s + 1) % N]).reshape(128, P, 4)
    rest = rng.permutation(P)[K // 2:]
    few[:, rest] = held.reshape(128, P, 4)[:, rest]
    x[(s + 1) % N] = few.reshape(128, 4 * P)
    return whole(x, hc, d["u"], d["w"])
def setup_inputs_one(rng):
    d = setup_inputs(rng)
    p, t = int(rng.integers(0, 128)), int(rng.integers(0, 4))
    u = np.zeros((N, 128, 512), BF)
    u[:, p, t] = -1.5
    off = np.sort(rng.permutation(P)[K // 2:])
    x, hc = np.array(d["x"]).reshape(N, 128, P, 4), np.array(d["hc"]).reshape(N, 128, P, 4)
    x[:, :, off[::2]] = (x[:, :, off[::2]].astype(np.float32) - np.float32(128)).astype(BF)
    x[:, p, off, t] = 0
    hc[:, p, off, t] = 0
    return whole(x.reshape(N, 128, 4 * P), hc.reshape(N, 128, 4 * P), u, d["w"])
def check_inputs(d):
    b = []
    for k, lo, hi in (("x", -16, 24), ("hl", -16, 24), ("hc", -16, 24), ("hr", -16, 24), ("u", -30, 30), ("w", -30, 30)):
        v = np.abs(d[k].astype(np.float32))
        if not (np.isfinite(v).all() and ((v == 0) | (v >= 2.0 ** lo) & (v <= 2.0 ** hi)).all()): b.append("a value of " + k)
    i = np.arange(N)
    hl, hc, hr, u = [d[k].astype(np.float32) for k in ("hl", "hc", "hr", "u")]
    if (hl != hc[(i - 1) % N]).any(): b.append("hl isn't the left neighbour's hc")
    if (hr != hc[(i + 1) % N]).any(): b.append("hr isn't the right neighbour's hc")
    if (u != u[:1]).any(): b.append("u isn't the same on all ranks")
    if (d["u"][:, :, 4:].astype(np.float32) != 0).any(): b.append("u has numbers behind its column 0")
    return b
def reference(x, hl, hc, hr, u, w):
    a, h, b = [[mx_ref.quantize(np.ascontiguousarray(v[r])) for r in range(N)] for v in (hl, hc, hr)]
    s = [x[r] for r in range(N)]
    ch = np.zeros((N, R, K), np.float32)
    for t in range(R):
        dh = decode(join(*h)).reshape(128, N, 4 * P).transpose(1, 0, 2)
        at, dq = [], []
        for r in range(N):
            v = ((dh[(r - 1) % N] + dh[(r + 1) % N]) - dh[r] * np.float32(2)) * np.float32(0.25)
            s[r] = (s[r].astype(np.float32) + v).astype(BF)
            q = mx_ref.quantize(np.ascontiguousarray((s[r].astype(np.float32) - dh[r]).astype(BF)))
            z = np.abs(mx_ref.matmul(mx_ref.quantize(np.ascontiguousarray(u[r])), q)[0]) + np.float32(0)
            e = np.argsort(-z, kind="stable")[:K]
            ch[r, t] = e
            at.append(e)
            dq.append(pick(q, e))
        dd = decode(join(*dq)).reshape(128, N, K, 4)
        for r in range(N):
            v = mx_ref.quantize(np.ascontiguousarray((dh[r].reshape(128, P, 4)[:, at[r]] + dd[:, r]).reshape(128, -1).astype(BF)))
            for held, o in ((a, (r + 1) % N), (h, r), (b, (r - 1) % N)): held[o] = put(held[o], at[r], v)
    oc, osc = np.zeros((N, 128, 12 * P), np.uint8), np.zeros((N, 16, 3 * P), np.uint8)
    y = np.zeros((N, 128, P), np.float32)
    for r in range(N):
        oc[r], osc[r] = emit(join(a[r], h[r], b[r]))
        y[r] = mx_ref.matmul(mx_ref.quantize(np.ascontiguousarray(w[r])), a[r])
    return {"oc": oc, "osc": osc, "xe": np.stack(s).astype(np.float32), "ch": ch, "y": y}

from concourse.bass import DstId, RemoteDMATransfer
from concourse.mybir import dt, AluOpType, AxisListType, ActivationFunctionType

P, K, R = 96, 16, 3
OWN, OH, AA, BB, LA, LB, WID = 128, 148, 288, 384, 512, 544, 576
NL = 3
NM = NL + K
PAT = OWN + NL
WA, WB = 288, 320
BASE = LA + NL - WA
SEL = 420
FAR = 512.0

SCRATCH = {}
for _n, _c, _d in (
        ("ones idn kk pm", 128, "bfloat16"), ("ubt win dr vt ct", 512, "bfloat16"), ("xin xn", 384, "bfloat16"),
        ("eb", 2048, "bfloat16"), ("hin", 1408, "bfloat16"), ("uin", 4, "bfloat16"), ("ot", 640, "bfloat16"),
        ("selt", 1024, "bfloat16"), ("wm", 6, "bfloat16"), ("cmp", 96, "bfloat16"),
        ("ipd ipe", 128, "int32"), ("ipx ilo ihi ipm", 1, "int32"), ("iwm iwn", 6, "int32"),
        ("fpm sj rk", 1, "float32"), ("jr jt fo", 80, "float32"), ("zf th sab dif yf", 96, "float32"), ("chs", 4, "float32"),
        ("xef", 384, "float32"), ("offp", 8, "uint16"), ("offh", 24, "uint16"), ("offn", 216, "uint16"),
        ("qe1 qe2 qe4", 512, "float8_e4m3fn_x4"), ("se1 se2 se4", 512, "uint8"), ("qs", 256, "float8_e4m3fn_x4"), ("ssl", 256, "uint8"),
        ("qu qw qc qd V0 V1 V2", 128, "float8_e4m3fn_x4"), ("su sw sc sd Z0 Z1 Z2", 128, "uint8"),
        ("W0 W1 W2 W3", WID, "float8_e4m3fn_x4"), ("S0 S1 S2 S3", WID, "uint8")):
    for _m in _n.split():
        SCRATCH[_m] = ("sbuf", [128, _c], _d)
for _b in range(4):
    SCRATCH["pv%d" % _b] = ("psum", [128, 512], "float32")
    SCRATCH["ph%d" % _b] = ("psum", [128, 512], "float32")

GAPS = ["gap%d" % _i for _i in range(10)]
SEMAPHORES = "sv sp ss sg loc out ldc ldl ldr ldx ldu ldw ra0 ra1 ra2 rb0 rb1 rb2".split() + GAPS

U8, U32 = dt.uint8, dt.uint32
OP, ACT = AluOpType, ActivationFunctionType


def four(n):
    return [(n + ".%d" % b, 0, 1) for b in range(4)]


def scheduler(g, T):
    queues = {"g": (g, "sg"), "v": (g.vector, "sv"), "p": (g.tensor, "sp"), "s": (g.scalar, "ss"), "y": (g.sync, None)}
    count, known, snap, log = {}, {q: {} for q in queues}, {}, {}

    def wait_for(q, deps):
        eng, own = queues[q]
        need = {}
        for s, v in deps:
            need[s] = max(need.get(s, 0), v)
        for s in sorted(need, key=lambda s: (s == own, s)):
            v = need[s]
            if known[q].get(s, 0) >= v:
                continue
            eng.wait_ge(T.sem[s], v)
            known[q][s] = v
            for s2, v2 in snap.get((s, v), {}).items():
                if known[q].get(s2, 0) < v2:
                    known[q][s2] = v2

    def find(reads, writes):
        deps = []
        for n, lo, hi in reads:
            deps += [tok for l, h, tok, w in log.get(n, []) if w and l < hi and lo < h]
        for n, lo, hi in writes:
            deps += [tok for l, h, tok, w in log.get(n, []) if l < hi and lo < h]
        return deps

    def note(reads, writes, tok):
        for n, lo, hi in reads:
            log.setdefault(n, []).append((lo, hi, tok, False))
        for n, lo, hi in writes:
            log[n] = [e for e in log.get(n, []) if not (lo <= e[0] and e[1] <= hi)] + [(lo, hi, tok, True)]

    def op(q, fn, reads, writes, chain=False):
        eng, own = queues[q]
        deps = find(reads, [])
        deps += [d for d in find([], writes) if not (chain and d[0] == own)]
        wait_for(q, deps)
        c = count[own] = count.get(own, 0) + 1
        fn(eng).then_inc(T.sem[own], 1)
        snap[(own, c)] = dict(known[q])
        note(reads, writes, (own, c))

    def dma(q, out, in_, reads, writes, sem):
        wait_for(q, find(reads, writes))
        c = count[sem] = count.get(sem, 0) + 16
        queues[q][0].dma_start(out, in_).then_inc(T.sem[sem], 16)
        snap[(sem, c)] = dict(known[q])
        note(reads, writes, (sem, c))

    def landed(writes, sem, v):
        note([], writes, (sem, v))

    def ready(q, reads):
        wait_for(q, find(reads, []))

    return op, dma, landed, ready, count


def rank_program(g, core, T, topo):
    rank = T.rank_of(core)
    if rank is None:
        return
    n = len(T.cores)
    right, left = T.cores[(rank + 1) % n], T.cores[(rank - 1) % n]
    op, dma, landed, ready, count = scheduler(g, T)

    def copy(out, in_, r, w):
        op("v", lambda e: e.tensor_copy(out, in_), r, w)

    def ts(out, in0, s1, s2, o0, o1, r, w):
        if o1 is None:
            op("v", lambda e: e.tensor_scalar(out, in0, s1, None, o0), r, w)
        else:
            op("v", lambda e: e.tensor_scalar(out, in0, s1, s2, o0, o1), r, w)

    def tt(out, a, b, o, r, w):
        op("v", lambda e: e.tensor_tensor(out, a, b, o), r, w)

    def act(out, in_, f, r, w, scale=1.0):
        if scale == 1.0:
            op("s", lambda e: e.activation(out, in_, f), r, w)
        else:
            op("s", lambda e: e.activation(out, in_, f, scale=scale), r, w)

    def quant(q, s, a, b, tile, r):
        op("v", lambda e: e.quantize_mx(T[q][:, a:b], T[s][:, a:b], tile), r, [(q, a, b), (s, a, b)])

    def mm(bank, lq, ls, la, rq, rs, ra, start, stop):
        l, r = slice(la, la + 128), slice(ra, ra + 128)
        op("p", lambda e: e.matmul_mx(T[bank][:, 0:128], T[lq][:, l], T[ls][:, l], T[rq][:, r], T[rs][:, r], start, stop),
           [(lq, la, la + 128), (ls, la, la + 128), (rq, ra, ra + 128), (rs, ra, ra + 128)], [(bank, 0, 512)], chain=not start)

    def fill(name, a, b, c, key=None):
        op("v", lambda e: e.memset(T[name][:, a:b], c), [], [key or (name, a, b)])

    def iota(name, a, b, pattern, base, cm, keys=None):
        if SCRATCH[name][2] == "int32":
            op("g", lambda e: e.iota(T[name][:, a:b], pattern, base, cm), [], [(name, a, b)])
        else:
            op("g", lambda e: e.iota(T[name][:, a:b], pattern, base, cm, allow_small_or_imprecise_dtypes=True), [], keys or [(name, a, b)])

    def unit(c, q, s):
        for b in range(4):
            ts(T.eb[:, 512 * b + b:512 * b + 512:4], T.idn[:], c, None, OP.mult, None, [("idn", 0, 128)], [("eb", 512 * b, 512 * b + 512)])
        quant(q, s, 0, 512, T.eb[:], [("eb", 0, 2048)])

    dma("y", T.hin[:, 0:384], T.hc[:], [], [("hin", 0, 384)], "ldc")
    dma("s", T.hin[:, 512:896], T.hl[:], [], [("hin", 512, 896)], "ldl")
    dma("y", T.hin[:, 896:1280], T.hr[:], [], [("hin", 896, 1280)], "ldr")
    dma("s", T.xin[:], T.x[:], [], [("xin", 0, 384)], "ldx")
    dma("y", T.uin[:], T.u[:, 0:4], [], [("uin", 0, 4)], "ldu")
    dma("y", T.win[:], T.w[:], [], [("win", 0, 512)], "ldw")

    fill("ones", 0, 128, 1.0)
    fill("eb", 0, 2048, 0.0)
    op("g", lambda e: e.affine_select(T.idn[:], T.ones[:], [[-1, 128]], OP.is_equal, 0.0, 0, 1), [("ones", 0, 128)], [("idn", 0, 128)])
    iota("ipx", 0, 1, [[0, 1]], 0, 1)
    iota("iwm", 0, 6, [[-16, 6]], 0, 1)
    iota("ct", 0, 512, [[0, 512]], 0, 0)
    iota("zf", 0, 96, [[0, 96]], 0, 0)
    op("g", lambda e: e.affine_select(T.th[:], T.zf[:], [[1, 96]], OP.is_ge, -1e-37, 0, -1), [("zf", 0, 96)], [("th", 0, 96)])
    iota("kk", 0, 128, [[0, 8], [1, 16]], 0, 0)
    iota("ot", 0, 640, [[0, 640]], 0, 0, four("ot"))
    iota("ipd", 0, 128, [[-1, 128]], 128, 1)
    iota("jr", 0, 64, [[0, 64]], 0, 0)
    iota("jr", 0, 6, [[16, 6]], AA - WA - BASE, 0)
    iota("jr", 64, 70, [[16, 6]], BB - WB - BASE, 0)
    iota("jr", 70, 76, [[16, 6]], 0 - PAT, 0)

    fill("hin", 384, 512, 0.0)
    fill("hin", 1280, 1408, 0.0)
    unit(1.0, "qe1", "se1")
    unit(-2.0, "qe2", "se2")
    quant("W0", "S0", 0, 128, T.hin[:, 0:512], [("hin", 0, 512)])
    quant("W0", "S0", AA, LA, T.hin[:, 512:1408], [("hin", 512, 1408)])
    act(T.xn[:], T.xin[:], ACT.Copy, [("xin", 0, 384)], four("xn"), scale=-4.0)

    gaps = list(GAPS)
    for t in range(R):
        for a, b in ([(BB + P, LA)] if t else []) + [(LA + NM, LB)]:
            for nm, cast in (("W", True), ("S", False)):
                src, dst = T[nm + "0"][:, BB + P:BB + P + b - a], T["%s%d" % (nm, t)][:, a:b]
                if cast:
                    src, dst = src.bitcast(U8), dst.bitcast(U8)
                dma("y", dst, src, [(nm + "0", BB + P, LA)], [("%s%d" % (nm, t), a, b)], gaps.pop())

    def held(t, bs, stop):
        w, s = "W%d" % t, "S%d" % t
        for b in bs:
            if t == 0:
                mm("ph%d" % b, "qe2", "se2", 128 * b, w, s, 0, True, False)
                mm("ph%d" % b, "qe2", "se2", 128 * b, w, s, 0, False, stop)
            else:
                mm("ph%d" % b, "qe4", "se4", 128 * b, w, s, 0, True, stop)

    def around(t):
        w, s = "W%d" % t, "S%d" % t
        for b in range(4):
            mm("pv%d" % b, "qe1", "se1", 128 * b, w, s, AA, True, False)
        for b in range(4):
            mm("pv%d" % b, "qe1", "se1", 128 * b, w, s, BB, False, False)
            mm("pv%d" % b, "qe2", "se2", 128 * b, w, s, 0, False, True)

    held(0, (0, 1), True)
    around(0)
    held(0, (2, 3), True)

    ts(T.ilo[:], T.ipx[:], 7, None, OP.bitwise_and, None, [("ipx", 0, 1)], [("ilo", 0, 1)])
    ts(T.ihi[:], T.ipx[:], 120, None, OP.bitwise_and, None, [("ipx", 0, 1)], [("ihi", 0, 1)])
    copy(T.ct[:, 0:1], T.ihi[:], [("ihi", 0, 1)], [("ct", 0, 1)])
    copy(T.ct[:, 4:5], T.ilo[:], [("ilo", 0, 1)], [("ct", 4, 5)])
    for b in range(4):
        ts(T.ubt[:, b:512:4], T.ones[:], T.uin[:, b:b + 1], None, OP.mult, None, [("ones", 0, 128), ("uin", 0, 4)], [("ubt.%d" % b, 0, 1)])
    quant("qu", "su", 0, 128, T.ubt[:], four("ubt"))
    quant("qc", "sc", 0, 128, T.ct[:], [("ct", 0, 512)])
    fill("dr", 384, 512, 0.0, ("dr.4", 0, 1))
    fill("vt", 384, 512, 0.0, ("vt.4", 0, 1))
    ts(T.iwn[:], T.iwm[:], 4, None, OP.arith_shift_right, None, [("iwm", 0, 6)], [("iwn", 0, 6)])
    ts(T.wm[:], T.iwn[:], 0.0, None, OP.is_equal, None, [("iwn", 0, 6)], [("wm", 0, 6)])

    for t in range(R):
        w, s, w1, s1 = "W%d" % t, "S%d" % t, "W%d" % (t + 1), "S%d" % (t + 1)
        v, z = "V%d" % t, "Z%d" % t
        last = t == R - 1

        def new_x(b):
            x = T.xn[:, b:384:4]
            tt(x, x, T["pv%d" % b][:, 0:P], OP.subtract, [("xn.%d" % b, 0, 1), ("pv%d" % b, 0, 512)], [("xn.%d" % b, 0, 1)])

        def drift(b):
            tt(T.dr[:, b:384:4], T.xn[:, b:384:4], T["ph%d" % b][:, 0:P], OP.subtract, [("xn.%d" % b, 0, 1), ("ph%d" % b, 0, 512)], [("dr.%d" % b, 0, 1)])

        new_x(0)
        new_x(1)
        drift(0)
        new_x(2)
        drift(1)
        new_x(3)
        drift(2)
        drift(3)
        quant("qd", "sd", 0, 128, T.dr[:], four("dr") + [("dr.4", 0, 1)])

        held(t, (0, 1, 2), False)
        mm("pv1", "qu", "su", 0, "qd", "sd", 0, True, True)
        mm("pv0", "qd", "sd", 0, "qu", "su", 0, True, True)
        held(t, (3,), False)
        for b in range(4):
            mm("ph%d" % b, "qe1", "se1", 128 * b, "qd", "sd", 0, False, True)
        act(T.sab[:], T.pv1[:, 0:P], ACT.Abs, [("pv1", 0, 512)], [("sab", 0, 96)])
        for b in range(4):
            act(T.vt[:, b:384:4], T["ph%d" % b][:, 0:P], ACT.Copy, [("ph%d" % b, 0, 512)], [("vt.%d" % b, 0, 1)], scale=-0.25)

        op("v", lambda e: e.tensor_reduce(T.sj[:], T.pv0[:, 0:1], AxisListType.X, OP.max, apply_absolute_value=True), [("pv0", 0, 512)], [("sj", 0, 1)])
        ts(T.dif[:], T.sab[:], T.sj[:], None, OP.subtract, None, [("sab", 0, 96), ("sj", 0, 1)], [("dif", 0, 96)])
        tt(T.cmp[:], T.dif[:], T.th[:], OP.is_gt, [("dif", 0, 96), ("th", 0, 96)], [("cmp", 0, 96)])
        op("v", lambda e: e.tensor_reduce(T.rk[:], T.cmp[:], AxisListType.X, OP.add), [("cmp", 0, 96)], [("rk", 0, 1)])
        o = 4 * (OH - OWN)
        ts(T.ot[:, o:o + 512:4], T.kk[:], T.rk[:], None, OP.is_equal, None, [("kk", 0, 128), ("rk", 0, 1)], [("ot.2", 0, 1)])
        ts(T.ot[:, 0:12:2], T.wm[:], T.rk[:], 16.0, OP.mult, OP.min, [("wm", 0, 6), ("rk", 0, 1)], [("ot.0", 0, 1)])
        ts(T.ot[:, 1:12:2], T.wm[:], T.rk[:], 16.0, OP.mult, OP.is_ge, [("wm", 0, 6), ("rk", 0, 1)], [("ot.1", 0, 1)])
        quant(w, s, OWN, OWN + 160, T.ot[:], four("ot"))
        mm("pv2", w, s, OH, "qc", "sc", 0, True, True)
        quant(v, z, 0, 128, T.vt[:], four("vt") + [("vt.4", 0, 1)])

        off, ko = T.offp[:, 2 * t:2 * t + 1], ("offp", 2 * t, 2 * t + 1)
        ts(off, T.pv2[:, 0:1], T.pv2[:, 1:2], None, OP.add, None, [("pv2", 0, 512)], [ko])
        copy(T[w][:, PAT:PAT + K].bitcast(U32), T[v][:, 0:128].bitcast(U32).indirect(off), [(v, 0, 128), ko], [(w, PAT, PAT + K)])
        act(T[s][:, PAT:PAT + K], T[z][:, 0:128].indirect(off), ACT.Copy, [(z, 0, 128), ko], [(s, PAT, PAT + K)])
        for nm, cast in ((w, True), (s, False)):
            ready("g", [(nm, OWN, OWN + NM)])
            trs = []
            for dst, col, sem, part in ((right, LA, "ra%d" % t, 0), (left, LB, "rb%d" % t, 1)):
                eng = topo.engines(core, dst)
                half = len(eng) // 2
                mask = sum(1 << e for e in eng[half * part:half * part + half])
                rid, pid = topo.addr(dst, core)
                a, b = T[nm][:, OWN:OWN + NM], T[nm][:, col:col + NM]
                if cast:
                    a, b = a.bitcast(U8), b.bitcast(U8)
                trs.append(RemoteDMATransfer(dst_ids=[DstId(rid=rid, pnc=pid)], dma_engine_mask=mask, remote_sem=T.sem[sem], src=a, dst=b))
                count["loc"] = count.get("loc", 0) + half
                count[sem] = count.get(sem, 0) + half
            g.remote_dma_fused(trs, local_sem=T.sem.loc)

        ts(T.chs[:, t:t + 1], T.pv2[:, 0:1], T.pv2[:, 1:2], None, OP.add, None, [("pv2", 0, 512)], [("chs", t, t + 1)])
        dma("y", T.ch[t:t + 1, :], T.chs[0:16, t:t + 1], [("chs", t, t + 1)], [], "out")
        if t == 0:
            fill("selt", 0, 1024, 0.0)
            ts(T.ipe[:], T.ipd[:], 15, None, OP.bitwise_and, None, [("ipd", 0, 128)], [("ipe", 0, 128)])
            ts(T.pm[:], T.ipe[:], 0.0, None, OP.is_equal, None, [("ipe", 0, 128)], [("pm", 0, 128)])
            for k in range(2):
                for i, c in ((0, 1.0), (1, -FAR)):
                    a = 512 * k + 2 * k + i
                    ts(T.selt[:, a:512 * k + 512:4], T.pm[:], c, None, OP.mult, None, [("pm", 0, 128), ("selt", 0, 1024)], [("selt.%d" % (2 * k + i), 0, 1)])
            quant("qs", "ssl", 0, 256, T.selt[:], four("selt"))
            ts(T.ipm[:], T.ipx[:], 15, None, OP.bitwise_and, None, [("ipx", 0, 1)], [("ipm", 0, 1)])
            copy(T.fpm[:], T.ipm[:], [("ipm", 0, 1)], [("fpm", 0, 1)])
            ts(T.jt[:, 0:76], T.jr[:, 0:76], T.fpm[:], None, OP.add, None, [("jr", 0, 76), ("fpm", 0, 1)], [("jt", 0, 76)])
            fill("offh", 0, 24, 0)
        for k in range(2):
            mm("pv%d" % k, "qs", "ssl", 128 * k, w, s, OWN, True, True)
        for k in range(2):
            tt(T.fo[:, 70 + k:76:2], T["pv%d" % k][:, 0:NL], T.jt[:, 70 + k:76:2], OP.max, [("pv%d" % k, 0, 512), ("jt", 0, 76)], [("fo.%d" % (2 + k), 0, 1)])
        ts(T.offh[:, 8 * t:8 * t + 6], T.fo[:, 70:76], float(PAT), None, OP.add, None, four("fo")[2:], [("offh", 8 * t, 8 * t + 6)])
        ho, hw = (AA + P, 96) if last else (0, 128)
        hl, ko = T.offh[:, 8 * t:8 * t + hw // 16], ("offh", 8 * t, 8 * t + 8)
        copy(T[w1][:, ho:ho + hw].bitcast(U32), T[w][:, 0:PAT + K].bitcast(U32).indirect(hl), [(w, 0, PAT + K), ko], [(w1, ho, ho + hw)])
        act(T[s1][:, ho:ho + hw], T[s][:, 0:PAT + K].indirect(hl), ACT.Copy, [(s, 0, PAT + K), ko], [(s1, ho, ho + hw)])
        if t == 0:
            unit(-4.0, "qe4", "se4")
        if t == 1:
            quant("qw", "sw", 0, 128, T.win[:], [("win", 0, 512)])

        def store(q, i, col):
            dma(q, T.oc[:, 4 * P * i:4 * P * i + 4 * P], T[w1][:, col:col + P].bitcast(U8), [(w1, col, col + P)], [], "out")

        def store_scales(q, i, col):
            for k in range(4):
                dma(q, T.osc[4 * k:4 * k + 4, P * i:P * i + P], T[s1][32 * k:32 * k + 4, col:col + P], [(s1, col, col + P)], [], "out")

        if last:
            act(T.xef[:], T.xn[:], ACT.Copy, four("xn"), [("xef", 0, 384)], scale=-0.25)
            dma("y", T.xe[:], T.xef[:], [("xef", 0, 384)], [], "out")
            store("y", 1, ho)
            store_scales("y", 1, ho)
        else:
            held(t + 1, range(4), True)

        landed([(w, LA, LA + NM), (s, LA, LA + NM)], "ra%d" % t, count["ra%d" % t])
        landed([(w, LB, LB + NM), (s, LB, LB + NM)], "rb%d" % t, count["rb%d" % t])
        for k in range(2):
            mm("pv%d" % (2 + k), "qs", "ssl", 128 * k, w, s, SEL, True, True)
        o = LA - SEL
        for k in range(2):
            tt(T.fo[:, k:70:2], T["pv%d" % (2 + k)][:, o:o + 35], T.jt[:, k:70:2], OP.max, [("pv%d" % (2 + k), 0, 512), ("jt", 0, 76)], [("fo.%d" % k, 0, 1)])
        ko = ("offn", 72 * t, 72 * t + 72)
        ts(T.offn[:, 72 * t:72 * t + 70], T.fo[:, 0:70], float(BASE), None, OP.add, None, four("fo")[:2], [ko])
        for i, (a, b, c) in enumerate(((WA, LA + NM, AA), (WB, LB + NM, AA + 2 * P if last else BB))):
            lst = T.offn[:, 72 * t + 64 * i:72 * t + 64 * i + 6]
            copy(T[w1][:, c:c + P].bitcast(U32), T[w][:, a:b].bitcast(U32).indirect(lst), [(w, a, b), ko], [(w1, c, c + P)])
            act(T[s1][:, c:c + P], T[s][:, a:b].indirect(lst), ACT.Copy, [(s, a, b), ko], [(s1, c, c + P)])
        if not last:
            around(t + 1)
        else:
            mm("pv0", "qw", "sw", 0, w1, s1, AA, True, True)
            copy(T.yf[:], T.pv0[:, 0:P], [("pv0", 0, 512)], [("yf", 0, 96)])
            store("y", 0, AA)
            store_scales("y", 0, AA)
            store_scales("s", 2, AA + 2 * P)
            store("y", 2, AA + 2 * P)
            dma("y", T.y[:], T.yf[:], [("yf", 0, 96)], [], "out")

    for sem in ("sv", "sp", "ss", "sg", "loc", "out"):
        g.wait_ge(T.sem[sem], count[sem])
